import numpy as np
import ml_dtypes


def mxq(x, axis, fmt="e4m3"):
    dtype, down = {"e4m3": (ml_dtypes.float8_e4m3fn, 7), "e5m2": (ml_dtypes.float8_e5m2, 14)}[fmt]
    v = np.moveaxis(np.asarray(x, np.float32).astype(ml_dtypes.bfloat16).astype(np.float64), axis, -1)
    blocks = v.reshape(v.shape[:-1] + (-1, 32))
    amax = np.abs(blocks).max(-1, keepdims=True)
    byte = np.maximum(np.where(amax > 0, np.frexp(amax)[1] - 1 + 127, 0) - down, 1)
    scale = np.exp2(byte - 127.0)
    codes = (blocks / scale).astype(np.float32).astype(dtype).astype(np.float64)
    return np.moveaxis((codes * scale).reshape(v.shape), -1, axis)


WIDE = False


def mx_kscale(k):
    if not WIDE:
        return np.ones(k)
    levels = np.array([10, -10, 5, -5, 0])
    if k % 512:
        return np.exp2(np.random.permutation(np.resize(levels, k // 32))).repeat(32)
    a = np.empty((k // 512, 16))
    for p in range(k // 512):
        a[p, :8] = np.random.permutation(np.resize(levels, 8))
        for g in range(8):
            far = levels[np.abs(levels - a[p, g]) >= 10]
            a[p, g + 8] = far[np.random.randint(len(far))]
    return np.exp2(a.ravel()).repeat(32)


def f64(x):
    return np.asarray(x).astype(np.float64)


E2M1 = np.array([0.0, 0.5, 1.0, 1.5, 2.0, 3.0, 4.0, 6.0, -0.0, -0.5, -1.0, -1.5, -2.0, -3.0, -4.0, -6.0])


def pack_weight(w, fmt):
    k, n = w.shape
    w = f64(np.asarray(w, np.float32).astype(ml_dtypes.bfloat16)).reshape(k // 32, 32, n)
    amax = np.abs(w).max(1)
    if fmt == "e4m3":
        byte = np.frexp(amax)[1] - 1 + 127 - 7
    else:
        mant, ex = np.frexp(amax / 6.0)
        byte = np.where(mant > 0.5, ex, ex - 1) + 127
    byte = np.clip(np.where(amax > 0, byte, 1), 1, 254)
    scaled = (w * np.exp2(127.0 - byte)[:, None, :]).reshape(k, n).astype(np.float32)
    by_word = np.ascontiguousarray(scaled.reshape(k // 512, 128, 4, n).transpose(0, 1, 3, 2))
    if fmt == "e4m3":
        words = by_word.astype(ml_dtypes.float8_e4m3fn).view(np.uint8)
    else:
        c = by_word.astype(ml_dtypes.float4_e2m1fn).view(np.uint8) & 0xF
        words = (c[..., 0::2] | (c[..., 1::2] << 4)).reshape(k // 512, 128, 2 * n)
    return np.ascontiguousarray(words), np.ascontiguousarray(byte.astype(np.uint8).reshape(k // 512, 16, n))


def unpack_weight(words, scales, fmt):
    g, _, n = scales.shape
    words = np.ascontiguousarray(words).reshape(g, 128, n, -1)
    if fmt == "e4m3":
        vals = words.view(ml_dtypes.float8_e4m3fn).astype(np.float64)
    else:
        nib = np.empty((g, 128, n, 4), np.uint8)
        nib[..., 0::2] = words & 0xF
        nib[..., 1::2] = words >> 4
        vals = E2M1[nib]
    vals = vals * np.repeat(np.exp2(scales.astype(np.float64) - 127.0), 8, axis=1)[..., None]
    return vals.transpose(0, 1, 3, 2).reshape(g * 512, n)


def bf(x):
    return np.asarray(x, np.float32).astype(ml_dtypes.bfloat16)


def planes(Y):
    r, m = Y.shape
    b = f64(bf(Y)).reshape(r // 32, 32, m)
    amax = np.abs(b).max(1)
    byte = np.clip(np.where(amax > 0, np.frexp(amax)[1] - 1 + 127 - 7, 1), 1, 254)
    codes = (b * np.exp2(127.0 - byte)[:, None, :]).reshape(r, m).astype(np.float32).astype(ml_dtypes.float8_e4m3fn).view(np.uint8)
    words = codes.reshape(r // 512, 128, 4, m).transpose(0, 1, 3, 2)
    return np.ascontiguousarray(words), np.ascontiguousarray(byte.astype(np.uint8).reshape(r // 512, 16, m))


K, L, M, T, B, N = 1024, 512, 512, 1024, 256, 512


def setup_inputs():
    n = np.random.standard_normal
    fk = mx_kscale(K)
    fl = mx_kscale(L)
    fm = mx_kscale(M)
    xtp = pack_weight(n((K, T)) / fk[:, None], "e2m1")
    wap = pack_weight(n((K, N)) * 1 / np.sqrt(K) * fk[:, None], "e4m3")
    wqp = pack_weight(n((L, N)) * 1 / np.sqrt(L) * fl[:, None], "e2m1")
    xgp = pack_weight(n((M, B)) / fm[:, None], "e4m3")
    return {
        "xt_words": xtp[0],
        "xt_scales": xtp[1],
        "wa_words": wap[0],
        "wa_scales": wap[1],
        "xq": (n((L, T)) / fl[:, None]).astype(np.float32),
        "wq_words": wqp[0],
        "wq_scales": wqp[1],
        "xg_words": xgp[0],
        "xg_scales": xgp[1],
        "wg": (n((M, N)) * 1 / np.sqrt(M) * fm[:, None]).astype(np.float32),
    }


def reference(xt_words, xt_scales, wa_words, wa_scales, xq, wq_words, wq_scales, xg_words, xg_scales, wg):
    xtu = unpack_weight(xt_words, xt_scales, "e2m1")
    wau = unpack_weight(wa_words, wa_scales, "e4m3")
    wqu = unpack_weight(wq_words, wq_scales, "e2m1")
    xgu = unpack_weight(xg_words, xg_scales, "e4m3")
    xqq = mxq(f64(xq), 0, "e4m3")
    z = wau.T @ xtu + wqu.T @ xqq
    mz = z.reshape(N, B, T // B).mean(axis=2)
    wgq = mxq(f64(wg), 0, "e4m3")
    g = wgq.T @ xgu
    s = mz + g
    sr = np.repeat(s, T // B, axis=1)
    y = 0.4 * z + np.maximum(sr, 0.0)
    words, scales = planes(y)
    return y, words, scales

@@ -1,0 +1,313 @@
+from contextlib import ExitStack
+
+import concourse.mybir as mybir
+
+K, L, M, T, B, N = 1024, 512, 512, 1024, 256, 512
+FLOPS = 2 * N * (K * T + L * T + M * B)
+
+F32 = mybir.dt.float32
+BF16 = mybir.dt.bfloat16
+I32 = mybir.dt.int32
+U32 = mybir.dt.uint32
+U8 = mybir.dt.uint8
+FP8X4 = mybir.dt.float8_e4m3fn_x4
+FP4X4 = mybir.dt.float4_e2m1fn_x4
+ALU = mybir.AluOpType
+ACT = mybir.ActivationFunctionType
+
+P = 128
+R = 4
+CH = 128
+PAIR = 256
+GRP = 4
+NPAIR = T // PAIR
+ZBANKS = 6
+
+
+def tile_mix_sum_shared_by_neighbours_pl_kernel(
+    tc, xt_words, xt_scales, wa_words, wa_scales, xq, wq_words, wq_scales, xg_words, xg_scales, wg, out_0, out_1, out_2
+):
+    nc = tc.nc
+    with ExitStack() as ctx:
+        sb = ctx.enter_context(tc.tile_pool(name="sb", bufs=1))
+        ps = ctx.enter_context(tc.psum_pool(name="ps", bufs=1))
+        ctx.enter_context(tc.manual_schedule())
+
+        def tile(name, shape, dtype):
+            return sb.tile(shape, dtype, name=name, align_bytes=64)
+
+        wa_raw = tile("wa_raw", [P, 2, N], I32)
+        wa_sc_raw = tile("wa_sc_raw", [P, 2, N], U8)
+        wq_raw = tile("wq_raw", [P, 2 * N], U8)
+        wq_sc_raw = tile("wq_sc_raw", [P, 1, N], U8)
+        wa_c = tile("wa_c", [P, 2, N], I32)
+        wa_s = tile("wa_s", [P, 2, N], U8)
+        wq_c = tile("wq_c", [P, 2 * N], U8)
+        wq_s = tile("wq_s", [P, N], U8)
+        xt_c = [tile("xt_c%d" % h, [P, 2, T], U8) for h in range(2)]
+        xt_s = tile("xt_s", [P, 2, T], U8)
+        xg_c = tile("xg_c", [P, B], I32)
+        xg_s = tile("xg_s", [P, 1, B], U8)
+        wg_raw = [tile("wg_raw%d" % h, [P, R, N // 2], F32) for h in range(2)]
+        wg_bf = tile("wg_bf", [P, R * N], BF16)
+        wg_c = tile("wg_c", [P, N], U32)
+        wg_s = tile("wg_s", [P, N], U8)
+        xq_raw = [tile("xq_raw%d" % k, [P, R, PAIR], F32) for k in range(NPAIR)]
+        xq_bf = [tile("xq_bf%d" % k, [P, R * PAIR], BF16) for k in range(NPAIR)]
+        xq_c = [tile("xq_c%d" % k, [P, PAIR], U32) for k in range(NPAIR)]
+        xq_s = [tile("xq_s%d" % k, [P, PAIR], U8) for k in range(NPAIR)]
+        sums = [tile("sums%d" % k, [P, R, PAIR // GRP], F32) for k in range(NPAIR)]
+        pre = [tile("pre%d" % k, [P, R, PAIR // GRP], F32) for k in range(NPAIR)]
+        shared = [tile("shared%d" % k, [P, 2, R, CH // GRP], F32) for k in range(NPAIR)]
+        y = [tile("y%d" % k, [P, R, PAIR], F32) for k in range(NPAIR)]
+        y_bf = [tile("y_bf%d" % k, [P, R * PAIR], BF16) for k in range(NPAIR)]
+        y_c = [tile("y_c%d" % k, [P, PAIR], U32) for k in range(NPAIR)]
+        y_s = tile("y_s", [P, T], U8)
+        g_ps = [ps.tile([P, R, CH], F32, name="g_ps%d" % h) for h in range(2)]
+        z_ps = {}
+
+        def load_scales(queue, plane, scales, quadrants=range(4)):
+            for q in quadrants:
+                queue.dma_start(
+                    out=plane[32 * q : 32 * q + 4].bitcast(I32),
+                    in_=scales[:, 4 * q : 4 * q + 4, :].rearrange("z r c -> r z c").bitcast(I32),
+                )
+
+        def load_xt(h):
+            nc.sync.dma_start(
+                out=xt_c[h][:].bitcast(I32),
+                in_=xt_words.rearrange("z p c -> p z c")[:, :, h * T : (h + 1) * T].bitcast(I32),
+            )
+
+        def load_rows(dst, src, c0, width):
+            nc.sync.dma_start(out=dst[:], in_=src.rearrange("(p j) c -> p j c", j=R)[:, :, c0 : c0 + width])
+
+        def interleaved(dst, src, c0, width):
+            d = dst[:, R * c0 : R * (c0 + width)].rearrange("p (c i j) -> p c j i", i=2, j=R)
+            s = src[:, :, c0 : c0 + width].rearrange("p j (c i) -> p c j i", i=2)
+            return d, s
+
+        def round_xq_scalar(k, c0, width):
+            d, s = interleaved(xq_bf[k], xq_raw[k], c0, width)
+            nc.scalar.activation(out=d, in_=s, func=ACT.Copy)
+
+        def round_xq_vector(k, c0, width):
+            d, s = interleaved(xq_bf[k], xq_raw[k], c0, width)
+            nc.vector.tensor_copy(out=d, in_=s)
+
+        def quant_xq(k, c0, width):
+            nc.vector.quantize_mx(
+                out=xq_c[k][:, c0 : c0 + width].bitcast(FP8X4),
+                scales=xq_s[k][:, c0 : c0 + width],
+                in_=xq_bf[k][:, R * c0 : R * (c0 + width)],
+            )
+
+        def round_wg(h):
+            half = P // 2
+            d = wg_bf[:].rearrange("p (r m j) -> p m j r", r=R, j=R)[:, h * half : (h + 1) * half]
+            s = wg_raw[h][:].rearrange("p j (m r) -> p m j r", r=R)
+            nc.scalar.activation(out=d, in_=s, func=ACT.Copy)
+
+        def z_first(c):
+            bank = ps.tile([P, R, CH], F32, name="z_ps%d" % c, tag="z%d" % (c % ZBANKS))
+            z_ps[c] = bank
+            h, cc = divmod(c, 4)
+            for z in range(2):
+                for r in range(R):
+                    nc.tensor.matmul_mx(
+                        out=bank[:, r, :],
+                        lhsT=wa_c[:, z, r * P : (r + 1) * P].bitcast(FP8X4),
+                        lhsT_scale=wa_s[:, z, r * P : (r + 1) * P],
+                        rhs=xt_c[h][:, z, 2 * CH * cc : 2 * CH * (cc + 1)].bitcast(FP4X4),
+                        rhs_scale=xt_s[:, z, CH * c : CH * (c + 1)],
+                        start=(z == 0 and r == 0),
+                        stop=False,
+                    )
+
+        def z_last(c):
+            k, h = divmod(c, 2)
+            for r in range(R):
+                nc.tensor.matmul_mx(
+                    out=z_ps[c][:, r, :],
+                    lhsT=wq_c[:, 2 * r * P : 2 * (r + 1) * P].bitcast(FP4X4),
+                    lhsT_scale=wq_s[:, r * P : (r + 1) * P],
+                    rhs=xq_c[k][:, CH * h : CH * (h + 1)].bitcast(FP8X4),
+                    rhs_scale=xq_s[k][:, CH * h : CH * (h + 1)],
+                    start=False,
+                    stop=(r == R - 1),
+                )
+
+        def g_product(h):
+            for r in range(R):
+                nc.tensor.matmul_mx(
+                    out=g_ps[h][:, r, :],
+                    lhsT=wg_c[:, r * P : (r + 1) * P].bitcast(FP8X4),
+                    lhsT_scale=wg_s[:, r * P : (r + 1) * P],
+                    rhs=xg_c[:, CH * h : CH * (h + 1)].bitcast(FP8X4),
+                    rhs_scale=xg_s[:, 0, CH * h : CH * (h + 1)],
+                    start=True,
+                    stop=True,
+                )
+
+        def group_sums(c):
+            k, h = divmod(c, 2)
+            nb = CH // GRP
+            nc.vector.tensor_reduce(
+                out=sums[k][:, :, nb * h : nb * (h + 1)],
+                in_=z_ps[c][:].rearrange("p r (b j) -> p r b j", j=GRP),
+                axis=mybir.AxisListType.X,
+                op=ALU.add,
+            )
+
+        def shared_part(k):
+            nb = PAIR // GRP
+            h, kk = divmod(k, 2)
+            nc.vector.scalar_tensor_tensor(
+                out=pre[k][:], in0=sums[k][:], scalar=1.0 / GRP, in1=g_ps[h][:, :, nb * kk : nb * (kk + 1)],
+                op0=ALU.mult, op1=ALU.add,
+            )
+            nc.scalar.activation(
+                out=shared[k][:].rearrange("p h r b -> p r h b"),
+                in_=pre[k][:].rearrange("p r (h b) -> p r h b", h=2),
+                func=ACT.Relu,
+            )
+
+        def result(c):
+            k, h = divmod(c, 2)
+            nc.vector.scalar_tensor_tensor(
+                out=y[k][:, :, CH * h : CH * (h + 1)].rearrange("p r (b j) -> p r b j", j=GRP),
+                in0=z_ps[c][:].rearrange("p r (b j) -> p r b j", j=GRP),
+                scalar=0.4,
+                in1=shared[k][:, h].unsqueeze(3).to_broadcast([P, R, CH // GRP, GRP]),
+                op0=ALU.mult, op1=ALU.add,
+            )
+
+        def store_y(k):
+            nc.sync.dma_start(out=out_0.rearrange("(p r) t -> p r t", r=R)[:, :, PAIR * k : PAIR * (k + 1)], in_=y[k][:])
+
+        def round_y_scalar(k, c0, width):
+            d, s = interleaved(y_bf[k], y[k], c0, width)
+            nc.scalar.copy(out=d, in_=s)
+
+        def round_y_vector(k, c0, width):
+            d, s = interleaved(y_bf[k], y[k], c0, width)
+            nc.vector.tensor_copy(out=d, in_=s)
+
+        def quant_y(k, c0, width):
+            nc.vector.quantize_mx(
+                out=y_c[k][:, c0 : c0 + width].bitcast(FP8X4),
+                scales=y_s[:, PAIR * k + c0 : PAIR * k + c0 + width],
+                in_=y_bf[k][:, R * c0 : R * (c0 + width)],
+            )
+
+        def store_words(k):
+            nc.sync.dma_start(
+                out=out_1[0].rearrange("p c r -> p (c r)")[:, R * PAIR * k : R * PAIR * (k + 1)].bitcast(I32),
+                in_=y_c[k][:].bitcast(I32),
+            )
+
+        nc.vector.memset(wa_sc_raw[:].bitcast(I32), 0)
+        nc.gpsimd.memset(xt_s[:].bitcast(I32), 0)
+        nc.vector.memset(wq_sc_raw[:].bitcast(I32), 0)
+        nc.vector.memset(xg_s[:].bitcast(I32), 0)
+        nc.sync.dma_start(out=wa_raw[:], in_=wa_words.rearrange("z p n r -> p z (n r)").bitcast(I32))
+        load_scales(nc.sync, wa_sc_raw, wa_scales)
+        load_xt(0)
+        load_scales(nc.sync, xt_s, xt_scales, range(2))
+        load_scales(nc.gpsimd, xt_s, xt_scales, range(2, 4))
+        load_rows(xq_raw[0], xq, 0, PAIR)
+        nc.sync.dma_start(out=wq_raw[:].bitcast(I32), in_=wq_words[0].bitcast(I32))
+        load_scales(nc.sync, wq_sc_raw, wq_scales)
+        load_scales(nc.gpsimd, xg_s, xg_scales)
+        load_rows(wg_raw[0], wg, 0, N // 2)
+        load_rows(xq_raw[1], xq, PAIR, PAIR)
+        load_rows(wg_raw[1], wg, N // 2, N // 2)
+        nc.sync.dma_start(out=xg_c[:], in_=xg_words[0].rearrange("p b r -> p (b r)").bitcast(I32))
+        load_xt(1)
+        load_rows(xq_raw[2], xq, 2 * PAIR, PAIR)
+        load_rows(xq_raw[3], xq, 3 * PAIR, PAIR)
+
+        nc.vector.tensor_copy(
+            out=wa_c[:].rearrange("p z (r m) -> p z m r", r=R), in_=wa_raw[:].rearrange("p z (m r) -> p z m r", r=R)
+        )
+        nc.vector.tensor_copy(
+            out=wa_s[:].rearrange("p z (r m) -> p z r m", r=R), in_=wa_sc_raw[:].rearrange("p z (m r) -> p z r m", r=R)
+        )
+        z_first(0)
+        z_first(1)
+        nc.vector.tensor_copy(
+            out=wq_c[:].rearrange("p (r m e) -> p r m e", r=R, e=2), in_=wq_raw[:].rearrange("p (m r e) -> p r m e", r=R, e=2)
+        )
+        round_xq_scalar(0, 0, CH)
+        round_xq_scalar(0, CH, CH)
+        nc.vector.tensor_copy(
+            out=wq_s[:].rearrange("p (r m) -> p r m", r=R), in_=wq_sc_raw[:, 0, :].rearrange("p (m r) -> p r m", r=R)
+        )
+        quant_xq(0, 0, CH)
+        quant_xq(0, CH, CH)
+        z_last(0)
+        z_last(1)
+        z_first(2)
+        z_first(3)
+        round_wg(0)
+        round_xq_scalar(1, 0, PAIR)
+        round_wg(1)
+        group_sums(0)
+        group_sums(1)
+        quant_xq(1, 0, PAIR)
+        z_last(2)
+        z_last(3)
+        z_first(4)
+        z_first(5)
+        group_sums(2)
+        nc.vector.quantize_mx(out=wg_c[:].bitcast(FP8X4), scales=wg_s[:], in_=wg_bf[:])
+        g_product(0)
+        g_product(1)
+        group_sums(3)
+        round_xq_scalar(2, 0, PAIR)
+        shared_part(0)
+        shared_part(1)
+        quant_xq(2, 0, PAIR)
+        z_last(4)
+        z_last(5)
+        result(0)
+        result(1)
+        store_y(0)
+        round_xq_scalar(3, 0, PAIR)
+        z_first(6)
+        z_first(7)
+        round_y_scalar(0, 0, PAIR)
+        group_sums(4)
+        group_sums(5)
+        quant_xq(3, 0, PAIR)
+        z_last(6)
+        z_last(7)
+        shared_part(2)
+        result(2)
+        result(3)
+        store_y(1)
+        round_y_scalar(1, 0, PAIR)
+        quant_y(0, 0, PAIR)
+        store_words(0)
+        group_sums(6)
+        group_sums(7)
+        result(4)
+        shared_part(3)
+        result(5)
+        store_y(2)
+        round_y_scalar(2, 0, PAIR)
+        quant_y(1, 0, PAIR)
+        store_words(1)
+        result(6)
+        round_y_scalar(3, 0, CH)
+        result(7)
+        store_y(3)
+        quant_y(2, 0, PAIR)
+        store_words(2)
+        round_y_vector(3, CH, CH)
+        quant_y(3, 0, CH)
+        quant_y(3, CH, CH)
+        store_words(3)
+        for q in range(4):
+            queue = nc.scalar if q < 2 else nc.sync
+            queue.dma_start(out=out_2[0, 4 * q : 4 * q + 4, :].bitcast(I32), in_=y_s[32 * q : 32 * q + 4, :].bitcast(I32))

@@ -16,12 +16,18 @@ ALU = mybir.AluOpType
 ACT = mybir.ActivationFunctionType
 
 P = 128
-R = 4
-CH = 128
-PAIR = 256
-GRP = 4
-NPAIR = T // PAIR
-ZBANKS = 6
+PACK = 4
+PASSES = K // (P * PACK)
+QUADRANTS = 4
+GROUP = T // B
+CHUNK = 128
+PAIR = 2 * CHUNK
+PAIRS = T // PAIR
+HALF_CHUNKS = T // CHUNK // 2
+Z_BANKS = 6
+Z_SCALE = 0.4
+WG_HALF = P // 2
+WG_SCALAR_SHARE = WG_HALF // 2
 
 
 def tile_mix_sum_shared_by_neighbours_pl_kernel(
@@ -29,285 +35,319 @@ def tile_mix_sum_shared_by_neighbours_pl_kernel(
 ):
     nc = tc.nc
     with ExitStack() as ctx:
-        sb = ctx.enter_context(tc.tile_pool(name="sb", bufs=1))
-        ps = ctx.enter_context(tc.psum_pool(name="ps", bufs=1))
+        sbuf = ctx.enter_context(tc.tile_pool(name="sbuf", bufs=1))
+        psum = ctx.enter_context(tc.psum_pool(name="psum", bufs=1))
         ctx.enter_context(tc.manual_schedule())
 
         def tile(name, shape, dtype):
-            return sb.tile(shape, dtype, name=name, align_bytes=64)
+            return sbuf.tile(shape, dtype, name=name, align_bytes=64)
 
-        wa_raw = tile("wa_raw", [P, 2, N], I32)
-        wa_sc_raw = tile("wa_sc_raw", [P, 2, N], U8)
+        def pair_tiles(name, shape, dtype):
+            return [tile("%s%d" % (name, k), shape, dtype) for k in range(PAIRS)]
+
+        wa_raw = tile("wa_raw", [P, PASSES, N], I32)
+        wa_raw_plane = tile("wa_raw_plane", [P, PASSES, N], U8)
         wq_raw = tile("wq_raw", [P, 2 * N], U8)
-        wq_sc_raw = tile("wq_sc_raw", [P, 1, N], U8)
-        wa_c = tile("wa_c", [P, 2, N], I32)
-        wa_s = tile("wa_s", [P, 2, N], U8)
-        wq_c = tile("wq_c", [P, 2 * N], U8)
-        wq_s = tile("wq_s", [P, N], U8)
-        xt_c = [tile("xt_c%d" % h, [P, 2, T], U8) for h in range(2)]
-        xt_s = tile("xt_s", [P, 2, T], U8)
-        xg_c = tile("xg_c", [P, B], I32)
-        xg_s = tile("xg_s", [P, 1, B], U8)
-        wg_raw = [tile("wg_raw%d" % h, [P, R, N // 2], F32) for h in range(2)]
-        wg_bf = tile("wg_bf", [P, R * N], BF16)
-        wg_c = tile("wg_c", [P, N], U32)
-        wg_s = tile("wg_s", [P, N], U8)
-        xq_raw = [tile("xq_raw%d" % k, [P, R, PAIR], F32) for k in range(NPAIR)]
-        xq_bf = [tile("xq_bf%d" % k, [P, R * PAIR], BF16) for k in range(NPAIR)]
-        xq_c = [tile("xq_c%d" % k, [P, PAIR], U32) for k in range(NPAIR)]
-        xq_s = [tile("xq_s%d" % k, [P, PAIR], U8) for k in range(NPAIR)]
-        sums = [tile("sums%d" % k, [P, R, PAIR // GRP], F32) for k in range(NPAIR)]
-        pre = [tile("pre%d" % k, [P, R, PAIR // GRP], F32) for k in range(NPAIR)]
-        shared = [tile("shared%d" % k, [P, 2, R, CH // GRP], F32) for k in range(NPAIR)]
-        y = [tile("y%d" % k, [P, R, PAIR], F32) for k in range(NPAIR)]
-        y_bf = [tile("y_bf%d" % k, [P, R * PAIR], BF16) for k in range(NPAIR)]
-        y_c = [tile("y_c%d" % k, [P, PAIR], U32) for k in range(NPAIR)]
-        y_s = tile("y_s", [P, T], U8)
-        g_ps = [ps.tile([P, R, CH], F32, name="g_ps%d" % h) for h in range(2)]
-        z_ps = {}
+        wq_raw_plane = tile("wq_raw_plane", [P, 1, N], U8)
+        wa_codes = tile("wa_codes", [P, PASSES, N], I32)
+        wa_plane = tile("wa_plane", [P, PASSES, N], U8)
+        wq_codes = tile("wq_codes", [P, 2 * N], U8)
+        wq_plane = tile("wq_plane", [P, N], U8)
+        xt_codes = [tile("xt_codes%d" % half, [P, PASSES, T], U8) for half in range(2)]
+        xt_plane = tile("xt_plane", [P, PASSES, T], U8)
+        xg_codes = tile("xg_codes", [P, B], I32)
+        xg_plane = tile("xg_plane", [P, 1, B], U8)
+        wg_raw = [tile("wg_raw%d" % half, [P, PACK, N // 2], F32) for half in range(2)]
+        wg_bf = tile("wg_bf", [P, PACK * N], BF16)
+        wg_codes = tile("wg_codes", [P, N], U32)
+        wg_plane = tile("wg_plane", [P, N], U8)
+        xq_raw = pair_tiles("xq_raw", [P, PACK, PAIR], F32)
+        xq_bf = pair_tiles("xq_bf", [P, PACK * PAIR], BF16)
+        xq_codes = pair_tiles("xq_codes", [P, PAIR], U32)
+        xq_plane = pair_tiles("xq_plane", [P, PAIR], U8)
+        sums = pair_tiles("sums", [P, PACK, PAIR // GROUP], F32)
+        s_tiles = pair_tiles("s", [P, PACK, PAIR // GROUP], F32)
+        shared = pair_tiles("shared", [P, 2, PACK, CHUNK // GROUP], F32)
+        y = pair_tiles("y", [P, PACK, PAIR], F32)
+        y_bf = pair_tiles("y_bf", [P, PACK * PAIR], BF16)
+        y_codes = tile("y_codes", [P, T], U32)
+        y_plane = tile("y_plane", [P, T], U8)
+        g_banks = [psum.tile([P, PACK, B // 2], F32, name="g_bank%d" % half) for half in range(2)]
+        z_banks = {}
+        z_scaled = {2 * k: tile("z_scaled%d" % (2 * k), [P, PACK, CHUNK], F32) for k in range(PAIRS - 1)}
 
-        def load_scales(queue, plane, scales, quadrants=range(4)):
-            for q in quadrants:
-                queue.dma_start(
+        def load_plane(plane, scales):
+            for q in range(QUADRANTS):
+                nc.sync.dma_start(
                     out=plane[32 * q : 32 * q + 4].bitcast(I32),
                     in_=scales[:, 4 * q : 4 * q + 4, :].rearrange("z r c -> r z c").bitcast(I32),
                 )
 
-        def load_xt(h):
+        def load_xt(half):
             nc.sync.dma_start(
-                out=xt_c[h][:].bitcast(I32),
-                in_=xt_words.rearrange("z p c -> p z c")[:, :, h * T : (h + 1) * T].bitcast(I32),
+                out=xt_codes[half][:].bitcast(I32),
+                in_=xt_words.rearrange("z p c -> p z c")[:, :, half * T : (half + 1) * T].bitcast(I32),
             )
 
-        def load_rows(dst, src, c0, width):
-            nc.sync.dma_start(out=dst[:], in_=src.rearrange("(p j) c -> p j c", j=R)[:, :, c0 : c0 + width])
+        def load_columns(dst, src, first, width):
+            nc.sync.dma_start(out=dst[:], in_=src.rearrange("(p j) c -> p j c", j=PACK)[:, :, first : first + width])
 
-        def interleaved(dst, src, c0, width):
-            d = dst[:, R * c0 : R * (c0 + width)].rearrange("p (c i j) -> p c j i", i=2, j=R)
-            s = src[:, :, c0 : c0 + width].rearrange("p j (c i) -> p c j i", i=2)
-            return d, s
+        def load_xq(k):
+            load_columns(xq_raw[k], xq, k * PAIR, PAIR)
 
-        def round_xq_scalar(k, c0, width):
-            d, s = interleaved(xq_bf[k], xq_raw[k], c0, width)
-            nc.scalar.activation(out=d, in_=s, func=ACT.Copy)
+        def load_wg(half):
+            load_columns(wg_raw[half], wg, half * N // 2, N // 2)
 
-        def round_xq_vector(k, c0, width):
-            d, s = interleaved(xq_bf[k], xq_raw[k], c0, width)
-            nc.vector.tensor_copy(out=d, in_=s)
-
-        def quant_xq(k, c0, width):
-            nc.vector.quantize_mx(
-                out=xq_c[k][:, c0 : c0 + width].bitcast(FP8X4),
-                scales=xq_s[k][:, c0 : c0 + width],
-                in_=xq_bf[k][:, R * c0 : R * (c0 + width)],
+        def interleaved(dst, src, first, width):
+            return (
+                dst[:, PACK * first : PACK * (first + width)].rearrange("p (c i j) -> p c j i", i=2, j=PACK),
+                src[:, :, first : first + width].rearrange("p j (c i) -> p c j i", i=2),
             )
 
-        def round_wg(h):
-            half = P // 2
-            d = wg_bf[:].rearrange("p (r m j) -> p m j r", r=R, j=R)[:, h * half : (h + 1) * half]
-            s = wg_raw[h][:].rearrange("p j (m r) -> p m j r", r=R)
-            nc.scalar.activation(out=d, in_=s, func=ACT.Copy)
+        def quantise(codes, plane, values):
+            nc.vector.quantize_mx(out=codes.bitcast(FP8X4), scales=plane, in_=values)
 
-        def z_first(c):
-            bank = ps.tile([P, R, CH], F32, name="z_ps%d" % c, tag="z%d" % (c % ZBANKS))
-            z_ps[c] = bank
-            h, cc = divmod(c, 4)
-            for z in range(2):
-                for r in range(R):
+        def round_xq(k, first=0, width=PAIR):
+            dst, src = interleaved(xq_bf[k], xq_raw[k], first, width)
+            nc.scalar.activation(out=dst, in_=src, func=ACT.Copy)
+
+        def quantise_xq(k, first=0, width=PAIR):
+            columns = slice(first, first + width)
+            quantise(xq_codes[k][:, columns], xq_plane[k][:, columns], xq_bf[k][:, PACK * first : PACK * (first + width)])
+
+        def round_wg(copy, half, first, last):
+            dst = wg_bf[:].rearrange("p (a e m j) -> p a m j e", a=2, e=2, j=PACK)
+            src = wg_raw[half][:].rearrange("p j (m a e) -> p a m j e", a=2, e=2)
+            copy(out=dst[:, :, half * WG_HALF + first : half * WG_HALF + last], in_=src[:, :, first:last])
+
+        def round_y(copy, k, first=0, width=PAIR):
+            dst, src = interleaved(y_bf[k], y[k], first, width)
+            copy(out=dst, in_=src)
+
+        def quantise_y(k, first=0, width=PAIR):
+            columns = slice(PAIR * k + first, PAIR * k + first + width)
+            quantise(y_codes[:, columns], y_plane[:, columns], y_bf[k][:, PACK * first : PACK * (first + width)])
+
+        def multiply_xt(c):
+            z_banks[c] = psum.tile([P, PACK, CHUNK], F32, name="z_bank%d" % c, tag="z%d" % (c % Z_BANKS))
+            half, chunk_in_half = divmod(c, HALF_CHUNKS)
+            for a in range(PASSES):
+                for r in range(PACK):
                     nc.tensor.matmul_mx(
-                        out=bank[:, r, :],
-                        lhsT=wa_c[:, z, r * P : (r + 1) * P].bitcast(FP8X4),
-                        lhsT_scale=wa_s[:, z, r * P : (r + 1) * P],
-                        rhs=xt_c[h][:, z, 2 * CH * cc : 2 * CH * (cc + 1)].bitcast(FP4X4),
-                        rhs_scale=xt_s[:, z, CH * c : CH * (c + 1)],
-                        start=(z == 0 and r == 0),
+                        out=z_banks[c][:, r, :],
+                        lhsT=wa_codes[:, a, r * P : (r + 1) * P].bitcast(FP8X4),
+                        lhsT_scale=wa_plane[:, a, r * P : (r + 1) * P],
+                        rhs=xt_codes[half][:, a, 2 * CHUNK * chunk_in_half : 2 * CHUNK * (chunk_in_half + 1)].bitcast(FP4X4),
+                        rhs_scale=xt_plane[:, a, CHUNK * c : CHUNK * (c + 1)],
+                        start=(a == 0 and r == 0),
                         stop=False,
                     )
 
-        def z_last(c):
+        def multiply_xq(c):
             k, h = divmod(c, 2)
-            for r in range(R):
+            for r in range(PACK):
                 nc.tensor.matmul_mx(
-                    out=z_ps[c][:, r, :],
-                    lhsT=wq_c[:, 2 * r * P : 2 * (r + 1) * P].bitcast(FP4X4),
-                    lhsT_scale=wq_s[:, r * P : (r + 1) * P],
-                    rhs=xq_c[k][:, CH * h : CH * (h + 1)].bitcast(FP8X4),
-                    rhs_scale=xq_s[k][:, CH * h : CH * (h + 1)],
+                    out=z_banks[c][:, r, :],
+                    lhsT=wq_codes[:, 2 * r * P : 2 * (r + 1) * P].bitcast(FP4X4),
+                    lhsT_scale=wq_plane[:, r * P : (r + 1) * P],
+                    rhs=xq_codes[k][:, CHUNK * h : CHUNK * (h + 1)].bitcast(FP8X4),
+                    rhs_scale=xq_plane[k][:, CHUNK * h : CHUNK * (h + 1)],
                     start=False,
-                    stop=(r == R - 1),
+                    stop=(r == PACK - 1),
                 )
 
-        def g_product(h):
-            for r in range(R):
+        def multiply_xg(half):
+            groups = slice(half * B // 2, (half + 1) * B // 2)
+            for r in range(PACK):
                 nc.tensor.matmul_mx(
-                    out=g_ps[h][:, r, :],
-                    lhsT=wg_c[:, r * P : (r + 1) * P].bitcast(FP8X4),
-                    lhsT_scale=wg_s[:, r * P : (r + 1) * P],
-                    rhs=xg_c[:, CH * h : CH * (h + 1)].bitcast(FP8X4),
-                    rhs_scale=xg_s[:, 0, CH * h : CH * (h + 1)],
+                    out=g_banks[half][:, r, :],
+                    lhsT=wg_codes[:, r * P : (r + 1) * P].bitcast(FP8X4),
+                    lhsT_scale=wg_plane[:, r * P : (r + 1) * P],
+                    rhs=xg_codes[:, groups].bitcast(FP8X4),
+                    rhs_scale=xg_plane[:, 0, groups],
                     start=True,
                     stop=True,
                 )
 
-        def group_sums(c):
+        def by_group(ap):
+            return ap.rearrange("p r (b j) -> p r b j", j=GROUP)
+
+        def sum_groups(c):
             k, h = divmod(c, 2)
-            nb = CH // GRP
+            width = CHUNK // GROUP
             nc.vector.tensor_reduce(
-                out=sums[k][:, :, nb * h : nb * (h + 1)],
-                in_=z_ps[c][:].rearrange("p r (b j) -> p r b j", j=GRP),
-                axis=mybir.AxisListType.X,
-                op=ALU.add,
+                out=sums[k][:, :, width * h : width * (h + 1)], in_=by_group(z_banks[c][:]), axis=mybir.AxisListType.X, op=ALU.add
             )
 
-        def shared_part(k):
-            nb = PAIR // GRP
-            h, kk = divmod(k, 2)
+        def make_s(k):
+            half, pair_in_half = divmod(k, 2)
+            width = PAIR // GROUP
             nc.vector.scalar_tensor_tensor(
-                out=pre[k][:], in0=sums[k][:], scalar=1.0 / GRP, in1=g_ps[h][:, :, nb * kk : nb * (kk + 1)],
-                op0=ALU.mult, op1=ALU.add,
+                out=s_tiles[k][:],
+                in0=sums[k][:],
+                scalar=1.0 / GROUP,
+                in1=g_banks[half][:, :, width * pair_in_half : width * (pair_in_half + 1)],
+                op0=ALU.mult,
+                op1=ALU.add,
             )
+
+        def make_shared(k):
             nc.scalar.activation(
                 out=shared[k][:].rearrange("p h r b -> p r h b"),
-                in_=pre[k][:].rearrange("p r (h b) -> p r h b", h=2),
+                in_=s_tiles[k][:].rearrange("p r (h b) -> p r h b", h=2),
                 func=ACT.Relu,
             )
 
-        def result(c):
+        def result_views(c):
             k, h = divmod(c, 2)
+            return (
+                by_group(y[k][:, :, CHUNK * h : CHUNK * (h + 1)]),
+                shared[k][:, h].unsqueeze(3).to_broadcast([P, PACK, CHUNK // GROUP, GROUP]),
+            )
+
+        def result_on_vector(c):
+            dst, repeated = result_views(c)
             nc.vector.scalar_tensor_tensor(
-                out=y[k][:, :, CH * h : CH * (h + 1)].rearrange("p r (b j) -> p r b j", j=GRP),
-                in0=z_ps[c][:].rearrange("p r (b j) -> p r b j", j=GRP),
-                scalar=0.4,
-                in1=shared[k][:, h].unsqueeze(3).to_broadcast([P, R, CH // GRP, GRP]),
-                op0=ALU.mult, op1=ALU.add,
+                out=dst, in0=by_group(z_banks[c][:]), scalar=Z_SCALE, in1=repeated, op0=ALU.mult, op1=ALU.add
             )
 
-        def store_y(k):
-            nc.sync.dma_start(out=out_0.rearrange("(p r) t -> p r t", r=R)[:, :, PAIR * k : PAIR * (k + 1)], in_=y[k][:])
+        def scale_z(c):
+            nc.scalar.activation(out=z_scaled[c][:], in_=z_banks[c][:], func=ACT.Copy, scale=Z_SCALE)
 
-        def round_y_scalar(k, c0, width):
-            d, s = interleaved(y_bf[k], y[k], c0, width)
-            nc.scalar.copy(out=d, in_=s)
+        def result_on_gpsimd(c):
+            dst, repeated = result_views(c)
+            nc.gpsimd.tensor_tensor(out=dst, in0=by_group(z_scaled[c][:]), in1=repeated, op=ALU.add)
 
-        def round_y_vector(k, c0, width):
-            d, s = interleaved(y_bf[k], y[k], c0, width)
-            nc.vector.tensor_copy(out=d, in_=s)
-
-        def quant_y(k, c0, width):
-            nc.vector.quantize_mx(
-                out=y_c[k][:, c0 : c0 + width].bitcast(FP8X4),
-                scales=y_s[:, PAIR * k + c0 : PAIR * k + c0 + width],
-                in_=y_bf[k][:, R * c0 : R * (c0 + width)],
-            )
-
-        def store_words(k):
+        def store_y(k, first=0, width=PAIR):
             nc.sync.dma_start(
-                out=out_1[0].rearrange("p c r -> p (c r)")[:, R * PAIR * k : R * PAIR * (k + 1)].bitcast(I32),
-                in_=y_c[k][:].bitcast(I32),
+                out=out_0.rearrange("(p r) t -> p r t", r=PACK)[:, :, PAIR * k + first : PAIR * k + first + width],
+                in_=y[k][:, :, first : first + width],
             )
 
-        nc.vector.memset(wa_sc_raw[:].bitcast(I32), 0)
-        nc.gpsimd.memset(xt_s[:].bitcast(I32), 0)
-        nc.vector.memset(wq_sc_raw[:].bitcast(I32), 0)
-        nc.vector.memset(xg_s[:].bitcast(I32), 0)
+        def store_codes(first_pair, end_pair):
+            nc.sync.dma_start(
+                out=out_1[0].rearrange("p c r -> p (c r)")[:, PACK * PAIR * first_pair : PACK * PAIR * end_pair].bitcast(I32),
+                in_=y_codes[:, PAIR * first_pair : PAIR * end_pair].bitcast(I32),
+            )
+
+        def store_plane():
+            for q in range(QUADRANTS):
+                queue = nc.scalar if q < QUADRANTS // 2 else nc.sync
+                queue.dma_start(
+                    out=out_2[0, 4 * q : 4 * q + 4, :].bitcast(I32), in_=y_plane[32 * q : 32 * q + 4, :].bitcast(I32)
+                )
+
+        nc.gpsimd.memset(wa_raw_plane[:].bitcast(I32), 0)
+        nc.vector.memset(xt_plane[:].bitcast(I32), 0)
+        nc.gpsimd.memset(xg_plane[:].bitcast(I32), 0)
+        nc.gpsimd.memset(wq_raw_plane[:].bitcast(I32), 0)
+
         nc.sync.dma_start(out=wa_raw[:], in_=wa_words.rearrange("z p n r -> p z (n r)").bitcast(I32))
-        load_scales(nc.sync, wa_sc_raw, wa_scales)
+        load_plane(wa_raw_plane, wa_scales)
+        load_xq(0)
         load_xt(0)
-        load_scales(nc.sync, xt_s, xt_scales, range(2))
-        load_scales(nc.gpsimd, xt_s, xt_scales, range(2, 4))
-        load_rows(xq_raw[0], xq, 0, PAIR)
         nc.sync.dma_start(out=wq_raw[:].bitcast(I32), in_=wq_words[0].bitcast(I32))
-        load_scales(nc.sync, wq_sc_raw, wq_scales)
-        load_scales(nc.gpsimd, xg_s, xg_scales)
-        load_rows(wg_raw[0], wg, 0, N // 2)
-        load_rows(xq_raw[1], xq, PAIR, PAIR)
-        load_rows(wg_raw[1], wg, N // 2, N // 2)
-        nc.sync.dma_start(out=xg_c[:], in_=xg_words[0].rearrange("p b r -> p (b r)").bitcast(I32))
+        load_plane(xt_plane, xt_scales)
+        load_xq(1)
+        load_plane(wq_raw_plane, wq_scales)
+        load_wg(0)
+        load_wg(1)
+        load_xq(2)
+        nc.sync.dma_start(out=xg_codes[:], in_=xg_words[0].rearrange("p b r -> p (b r)").bitcast(I32))
+        load_plane(xg_plane, xg_scales)
         load_xt(1)
-        load_rows(xq_raw[2], xq, 2 * PAIR, PAIR)
-        load_rows(xq_raw[3], xq, 3 * PAIR, PAIR)
+        load_xq(3)
 
         nc.vector.tensor_copy(
-            out=wa_c[:].rearrange("p z (r m) -> p z m r", r=R), in_=wa_raw[:].rearrange("p z (m r) -> p z m r", r=R)
+            out=wa_codes[:].rearrange("p z (a e m) -> p z a m e", a=2, e=2),
+            in_=wa_raw[:].rearrange("p z (m a e) -> p z a m e", a=2, e=2),
         )
         nc.vector.tensor_copy(
-            out=wa_s[:].rearrange("p z (r m) -> p z r m", r=R), in_=wa_sc_raw[:].rearrange("p z (m r) -> p z r m", r=R)
+            out=wa_plane[:].rearrange("p z (r m) -> p z r m", r=PACK),
+            in_=wa_raw_plane[:].rearrange("p z (m r) -> p z r m", r=PACK),
         )
-        z_first(0)
-        z_first(1)
+        for h in range(2):
+            round_xq(0, h * CHUNK, CHUNK)
         nc.vector.tensor_copy(
-            out=wq_c[:].rearrange("p (r m e) -> p r m e", r=R, e=2), in_=wq_raw[:].rearrange("p (m r e) -> p r m e", r=R, e=2)
+            out=wq_codes[:].rearrange("p (r m e) -> p r m e", r=PACK, e=2),
+            in_=wq_raw[:].rearrange("p (m r e) -> p r m e", r=PACK, e=2),
         )
-        round_xq_scalar(0, 0, CH)
-        round_xq_scalar(0, CH, CH)
+        for h in range(2):
+            quantise_xq(0, h * CHUNK, CHUNK)
         nc.vector.tensor_copy(
-            out=wq_s[:].rearrange("p (r m) -> p r m", r=R), in_=wq_sc_raw[:, 0, :].rearrange("p (m r) -> p r m", r=R)
+            out=wq_plane[:].rearrange("p (r m) -> p r m", r=PACK),
+            in_=wq_raw_plane[:, 0, :].rearrange("p (m r) -> p r m", r=PACK),
         )
-        quant_xq(0, 0, CH)
-        quant_xq(0, CH, CH)
-        z_last(0)
-        z_last(1)
-        z_first(2)
-        z_first(3)
-        round_wg(0)
-        round_xq_scalar(1, 0, PAIR)
-        round_wg(1)
-        group_sums(0)
-        group_sums(1)
-        quant_xq(1, 0, PAIR)
-        z_last(2)
-        z_last(3)
-        z_first(4)
-        z_first(5)
-        group_sums(2)
-        nc.vector.quantize_mx(out=wg_c[:].bitcast(FP8X4), scales=wg_s[:], in_=wg_bf[:])
-        g_product(0)
-        g_product(1)
-        group_sums(3)
-        round_xq_scalar(2, 0, PAIR)
-        shared_part(0)
-        shared_part(1)
-        quant_xq(2, 0, PAIR)
-        z_last(4)
-        z_last(5)
-        result(0)
-        result(1)
-        store_y(0)
-        round_xq_scalar(3, 0, PAIR)
-        z_first(6)
-        z_first(7)
-        round_y_scalar(0, 0, PAIR)
-        group_sums(4)
-        group_sums(5)
-        quant_xq(3, 0, PAIR)
-        z_last(6)
-        z_last(7)
-        shared_part(2)
-        result(2)
-        result(3)
-        store_y(1)
-        round_y_scalar(1, 0, PAIR)
-        quant_y(0, 0, PAIR)
-        store_words(0)
-        group_sums(6)
-        group_sums(7)
-        result(4)
-        shared_part(3)
-        result(5)
-        store_y(2)
-        round_y_scalar(2, 0, PAIR)
-        quant_y(1, 0, PAIR)
-        store_words(1)
-        result(6)
-        round_y_scalar(3, 0, CH)
-        result(7)
-        store_y(3)
-        quant_y(2, 0, PAIR)
-        store_words(2)
-        round_y_vector(3, CH, CH)
-        quant_y(3, 0, CH)
-        quant_y(3, CH, CH)
-        store_words(3)
-        for q in range(4):
-            queue = nc.scalar if q < 2 else nc.sync
-            queue.dma_start(out=out_2[0, 4 * q : 4 * q + 4, :].bitcast(I32), in_=y_s[32 * q : 32 * q + 4, :].bitcast(I32))
+
+        multiply_xt(0)
+        multiply_xt(1)
+        multiply_xq(0)
+        multiply_xq(1)
+        round_xq(1)
+        quantise_xq(1)
+        for c in (2, 3):
+            multiply_xt(c)
+            multiply_xq(c)
+
+        round_wg(nc.scalar.copy, 0, 0, WG_HALF)
+        round_wg(nc.scalar.copy, 1, 0, WG_SCALAR_SHARE)
+        sum_groups(0)
+        sum_groups(1)
+        round_wg(nc.vector.tensor_copy, 1, WG_SCALAR_SHARE, WG_HALF)
+        sum_groups(2)
+        quantise(wg_codes[:], wg_plane[:], wg_bf[:])
+        multiply_xg(0)
+        multiply_xt(4)
+        multiply_xt(5)
+        scale_z(0)
+        round_xq(2)
+        sum_groups(3)
+
+        make_s(0)
+        make_shared(0)
+        quantise_xq(2)
+        multiply_xq(4)
+        multiply_xq(5)
+        multiply_xg(1)
+        multiply_xt(6)
+        make_s(1)
+        scale_z(2)
+        make_shared(1)
+        round_xq(3)
+
+        for k in range(PAIRS - 1):
+            result_on_gpsimd(2 * k)
+            if k > 0:
+                sum_groups(2 * k + 2)
+                sum_groups(2 * k + 3)
+            result_on_vector(2 * k + 1)
+            store_y(k)
+            if k == 0:
+                multiply_xt(7)
+            if k == 1:
+                quantise_xq(3)
+                multiply_xq(6)
+                multiply_xq(7)
+                scale_z(4)
+            if k > 0:
+                make_s(k + 1)
+                make_shared(k + 1)
+            round_y(nc.scalar.copy, k)
+            if k > 0:
+                quantise_y(k - 1)
+            if k == 1:
+                store_codes(0, 1)
+
+        last = PAIRS - 1
+        result_on_vector(2 * last)
+        store_y(last, 0, CHUNK)
+        round_y(nc.scalar.copy, last, 0, CHUNK)
+        result_on_vector(2 * last + 1)
+        store_y(last, CHUNK, CHUNK)
+        quantise_y(last - 1)
+        store_codes(1, last)
+        round_y(nc.vector.tensor_copy, last, CHUNK, CHUNK)
+        for h in range(2):
+            quantise_y(last, h * CHUNK, CHUNK)
+        store_codes(last, PAIRS)
+        store_plane()

@@ -76,9 +76,9 @@ def tile_mix_sum_shared_by_neighbours_pl_kernel(
         z_banks = {}
         z_scaled = {2 * k: tile("z_scaled%d" % (2 * k), [P, PACK, CHUNK], F32) for k in range(PAIRS - 1)}
 
-        def load_plane(plane, scales):
-            for q in range(QUADRANTS):
-                nc.sync.dma_start(
+        def load_plane(plane, scales, queue=nc.sync, quadrants=range(QUADRANTS)):
+            for q in quadrants:
+                queue.dma_start(
                     out=plane[32 * q : 32 * q + 4].bitcast(I32),
                     in_=scales[:, 4 * q : 4 * q + 4, :].rearrange("z r c -> r z c").bitcast(I32),
                 )
@@ -120,13 +120,13 @@ def tile_mix_sum_shared_by_neighbours_pl_kernel(
             src = wg_raw[half][:].rearrange("p j (m a e) -> p a m j e", a=2, e=2)
             copy(out=dst[:, :, half * WG_HALF + first : half * WG_HALF + last], in_=src[:, :, first:last])
 
-        def round_y(copy, k, first=0, width=PAIR):
-            dst, src = interleaved(y_bf[k], y[k], first, width)
+        def round_y(copy, k):
+            dst, src = interleaved(y_bf[k], y[k], 0, PAIR)
             copy(out=dst, in_=src)
 
-        def quantise_y(k, first=0, width=PAIR):
-            columns = slice(PAIR * k + first, PAIR * k + first + width)
-            quantise(y_codes[:, columns], y_plane[:, columns], y_bf[k][:, PACK * first : PACK * (first + width)])
+        def quantise_y(k):
+            columns = slice(PAIR * k, PAIR * (k + 1))
+            quantise(y_codes[:, columns], y_plane[:, columns], y_bf[k][:])
 
         def multiply_xt(c):
             z_banks[c] = psum.tile([P, PACK, CHUNK], F32, name="z_bank%d" % c, tag="z%d" % (c % Z_BANKS))
@@ -218,11 +218,8 @@ def tile_mix_sum_shared_by_neighbours_pl_kernel(
             dst, repeated = result_views(c)
             nc.gpsimd.tensor_tensor(out=dst, in0=by_group(z_scaled[c][:]), in1=repeated, op=ALU.add)
 
-        def store_y(k, first=0, width=PAIR):
-            nc.sync.dma_start(
-                out=out_0.rearrange("(p r) t -> p r t", r=PACK)[:, :, PAIR * k + first : PAIR * k + first + width],
-                in_=y[k][:, :, first : first + width],
-            )
+        def store_y(k):
+            nc.sync.dma_start(out=out_0.rearrange("(p r) t -> p r t", r=PACK)[:, :, PAIR * k : PAIR * (k + 1)], in_=y[k][:])
 
         def store_codes(first_pair, end_pair):
             nc.sync.dma_start(
@@ -247,9 +244,10 @@ def tile_mix_sum_shared_by_neighbours_pl_kernel(
         load_xq(0)
         load_xt(0)
         nc.sync.dma_start(out=wq_raw[:].bitcast(I32), in_=wq_words[0].bitcast(I32))
+        load_plane(wq_raw_plane, wq_scales, nc.gpsimd, range(QUADRANTS // 2, QUADRANTS))
         load_plane(xt_plane, xt_scales)
         load_xq(1)
-        load_plane(wq_raw_plane, wq_scales)
+        load_plane(wq_raw_plane, wq_scales, nc.sync, range(QUADRANTS // 2))
         load_wg(0)
         load_wg(1)
         load_xq(2)
@@ -311,43 +309,47 @@ def tile_mix_sum_shared_by_neighbours_pl_kernel(
         multiply_xg(1)
         multiply_xt(6)
         make_s(1)
-        scale_z(2)
         make_shared(1)
         round_xq(3)
+        scale_z(2)
 
-        for k in range(PAIRS - 1):
-            result_on_gpsimd(2 * k)
-            if k > 0:
-                sum_groups(2 * k + 2)
-                sum_groups(2 * k + 3)
-            result_on_vector(2 * k + 1)
-            store_y(k)
-            if k == 0:
-                multiply_xt(7)
-            if k == 1:
-                quantise_xq(3)
-                multiply_xq(6)
-                multiply_xq(7)
-                scale_z(4)
-            if k > 0:
-                make_s(k + 1)
-                make_shared(k + 1)
-            round_y(nc.scalar.copy, k)
-            if k > 0:
-                quantise_y(k - 1)
-            if k == 1:
-                store_codes(0, 1)
+        result_on_gpsimd(0)
+        result_on_vector(1)
+        store_y(0)
+        multiply_xt(7)
+        sum_groups(4)
+        sum_groups(5)
+        quantise_xq(3)
+        multiply_xq(6)
+        multiply_xq(7)
 
-        last = PAIRS - 1
-        result_on_vector(2 * last)
-        store_y(last, 0, CHUNK)
-        round_y(nc.scalar.copy, last, 0, CHUNK)
-        result_on_vector(2 * last + 1)
-        store_y(last, CHUNK, CHUNK)
-        quantise_y(last - 1)
-        store_codes(1, last)
-        round_y(nc.vector.tensor_copy, last, CHUNK, CHUNK)
-        for h in range(2):
-            quantise_y(last, h * CHUNK, CHUNK)
-        store_codes(last, PAIRS)
+        result_on_gpsimd(2)
+        result_on_vector(3)
+        store_y(1)
+        scale_z(4)
+        make_s(2)
+        make_shared(2)
+        round_y(nc.scalar.copy, 0)
+
+        result_on_gpsimd(4)
+        sum_groups(6)
+        sum_groups(7)
+        make_s(3)
+        make_shared(3)
+        round_y(nc.scalar.copy, 1)
+        result_on_vector(5)
+        store_y(2)
+        round_y(nc.scalar.copy, 2)
+
+        result_on_vector(6)
+        result_on_vector(7)
+        store_y(3)
+
+        quantise_y(0)
+        quantise_y(1)
+        store_codes(0, 2)
+        round_y(nc.vector.tensor_copy, 3)
+        quantise_y(2)
+        quantise_y(3)
+        store_codes(2, PAIRS)
         store_plane()

from contextlib import ExitStack

import concourse.mybir as mybir

K, L, M, T, B, N = 1024, 512, 512, 1024, 256, 512
FLOPS = 2 * N * (K * T + L * T + M * B)

F32 = mybir.dt.float32
BF16 = mybir.dt.bfloat16
I32 = mybir.dt.int32
U32 = mybir.dt.uint32
U8 = mybir.dt.uint8
FP8X4 = mybir.dt.float8_e4m3fn_x4
FP4X4 = mybir.dt.float4_e2m1fn_x4
ALU = mybir.AluOpType
ACT = mybir.ActivationFunctionType

P = 128
PACK = 4
PASSES = K // (P * PACK)
QUADRANTS = 4
GROUP = T // B
CHUNK = 128
PAIR = 2 * CHUNK
PAIRS = T // PAIR
HALF_CHUNKS = T // CHUNK // 2
Z_BANKS = 6
Z_SCALE = 0.4
WG_HALF = P // 2
WG_SCALAR_SHARE = WG_HALF // 2


def tile_mix_sum_shared_by_neighbours_pl_kernel(
    tc, xt_words, xt_scales, wa_words, wa_scales, xq, wq_words, wq_scales, xg_words, xg_scales, wg, out_0, out_1, out_2
):
    nc = tc.nc
    with ExitStack() as ctx:
        sbuf = ctx.enter_context(tc.tile_pool(name="sbuf", bufs=1))
        psum = ctx.enter_context(tc.psum_pool(name="psum", bufs=1))
        ctx.enter_context(tc.manual_schedule())

        def tile(name, shape, dtype):
            return sbuf.tile(shape, dtype, name=name, align_bytes=64)

        def pair_tiles(name, shape, dtype):
            return [tile("%s%d" % (name, k), shape, dtype) for k in range(PAIRS)]

        wa_raw = tile("wa_raw", [P, PASSES, N], I32)
        wa_raw_plane = tile("wa_raw_plane", [P, PASSES, N], U8)
        wq_raw = tile("wq_raw", [P, 2 * N], U8)
        wq_raw_plane = tile("wq_raw_plane", [P, 1, N], U8)
        wa_codes = tile("wa_codes", [P, PASSES, N], I32)
        wa_plane = tile("wa_plane", [P, PASSES, N], U8)
        wq_codes = tile("wq_codes", [P, 2 * N], U8)
        wq_plane = tile("wq_plane", [P, N], U8)
        xt_codes = [tile("xt_codes%d" % half, [P, PASSES, T], U8) for half in range(2)]
        xt_plane = tile("xt_plane", [P, PASSES, T], U8)
        xg_codes = tile("xg_codes", [P, B], I32)
        xg_plane = tile("xg_plane", [P, 1, B], U8)
        wg_raw = [tile("wg_raw%d" % half, [P, PACK, N // 2], F32) for half in range(2)]
        wg_bf = tile("wg_bf", [P, PACK * N], BF16)
        wg_codes = tile("wg_codes", [P, N], U32)
        wg_plane = tile("wg_plane", [P, N], U8)
        xq_raw = pair_tiles("xq_raw", [P, PACK, PAIR], F32)
        xq_bf = pair_tiles("xq_bf", [P, PACK * PAIR], BF16)
        xq_codes = pair_tiles("xq_codes", [P, PAIR], U32)
        xq_plane = pair_tiles("xq_plane", [P, PAIR], U8)
        sums = pair_tiles("sums", [P, PACK, PAIR // GROUP], F32)
        s_tiles = pair_tiles("s", [P, PACK, PAIR // GROUP], F32)
        shared = pair_tiles("shared", [P, 2, PACK, CHUNK // GROUP], F32)
        y = pair_tiles("y", [P, PACK, PAIR], F32)
        y_bf = pair_tiles("y_bf", [P, PACK * PAIR], BF16)
        y_codes = tile("y_codes", [P, T], U32)
        y_plane = tile("y_plane", [P, T], U8)
        g_banks = [psum.tile([P, PACK, B // 2], F32, name="g_bank%d" % half) for half in range(2)]
        z_banks = {}
        z_scaled = {2 * k: tile("z_scaled%d" % (2 * k), [P, PACK, CHUNK], F32) for k in range(PAIRS - 1)}

        def load_plane(plane, scales, queue=nc.sync, quadrants=range(QUADRANTS)):
            for q in quadrants:
                queue.dma_start(
                    out=plane[32 * q : 32 * q + 4].bitcast(I32),
                    in_=scales[:, 4 * q : 4 * q + 4, :].rearrange("z r c -> r z c").bitcast(I32),
                )

        def load_xt(half):
            nc.sync.dma_start(
                out=xt_codes[half][:].bitcast(I32),
                in_=xt_words.rearrange("z p c -> p z c")[:, :, half * T : (half + 1) * T].bitcast(I32),
            )

        def load_columns(dst, src, first, width):
            nc.sync.dma_start(out=dst[:], in_=src.rearrange("(p j) c -> p j c", j=PACK)[:, :, first : first + width])

        def load_xq(k):
            load_columns(xq_raw[k], xq, k * PAIR, PAIR)

        def load_wg(half):
            load_columns(wg_raw[half], wg, half * N // 2, N // 2)

        def interleaved(dst, src, first, width):
            return (
                dst[:, PACK * first : PACK * (first + width)].rearrange("p (c i j) -> p c j i", i=2, j=PACK),
                src[:, :, first : first + width].rearrange("p j (c i) -> p c j i", i=2),
            )

        def quantise(codes, plane, values):
            nc.vector.quantize_mx(out=codes.bitcast(FP8X4), scales=plane, in_=values)

        def round_xq(k, first=0, width=PAIR):
            dst, src = interleaved(xq_bf[k], xq_raw[k], first, width)
            nc.scalar.activation(out=dst, in_=src, func=ACT.Copy)

        def quantise_xq(k, first=0, width=PAIR):
            columns = slice(first, first + width)
            quantise(xq_codes[k][:, columns], xq_plane[k][:, columns], xq_bf[k][:, PACK * first : PACK * (first + width)])

        def round_wg(copy, half, first, last):
            dst = wg_bf[:].rearrange("p (a e m j) -> p a m j e", a=2, e=2, j=PACK)
            src = wg_raw[half][:].rearrange("p j (m a e) -> p a m j e", a=2, e=2)
            copy(out=dst[:, :, half * WG_HALF + first : half * WG_HALF + last], in_=src[:, :, first:last])

        def round_y(copy, k):
            dst, src = interleaved(y_bf[k], y[k], 0, PAIR)
            copy(out=dst, in_=src)

        def quantise_y(k):
            columns = slice(PAIR * k, PAIR * (k + 1))
            quantise(y_codes[:, columns], y_plane[:, columns], y_bf[k][:])

        def multiply_xt(c):
            z_banks[c] = psum.tile([P, PACK, CHUNK], F32, name="z_bank%d" % c, tag="z%d" % (c % Z_BANKS))
            half, chunk_in_half = divmod(c, HALF_CHUNKS)
            for a in range(PASSES):
                for r in range(PACK):
                    nc.tensor.matmul_mx(
                        out=z_banks[c][:, r, :],
                        lhsT=wa_codes[:, a, r * P : (r + 1) * P].bitcast(FP8X4),
                        lhsT_scale=wa_plane[:, a, r * P : (r + 1) * P],
                        rhs=xt_codes[half][:, a, 2 * CHUNK * chunk_in_half : 2 * CHUNK * (chunk_in_half + 1)].bitcast(FP4X4),
                        rhs_scale=xt_plane[:, a, CHUNK * c : CHUNK * (c + 1)],
                        start=(a == 0 and r == 0),
                        stop=False,
                    )

        def multiply_xq(c):
            k, h = divmod(c, 2)
            for r in range(PACK):
                nc.tensor.matmul_mx(
                    out=z_banks[c][:, r, :],
                    lhsT=wq_codes[:, 2 * r * P : 2 * (r + 1) * P].bitcast(FP4X4),
                    lhsT_scale=wq_plane[:, r * P : (r + 1) * P],
                    rhs=xq_codes[k][:, CHUNK * h : CHUNK * (h + 1)].bitcast(FP8X4),
                    rhs_scale=xq_plane[k][:, CHUNK * h : CHUNK * (h + 1)],
                    start=False,
                    stop=(r == PACK - 1),
                )

        def multiply_xg(half):
            groups = slice(half * B // 2, (half + 1) * B // 2)
            for r in range(PACK):
                nc.tensor.matmul_mx(
                    out=g_banks[half][:, r, :],
                    lhsT=wg_codes[:, r * P : (r + 1) * P].bitcast(FP8X4),
                    lhsT_scale=wg_plane[:, r * P : (r + 1) * P],
                    rhs=xg_codes[:, groups].bitcast(FP8X4),
                    rhs_scale=xg_plane[:, 0, groups],
                    start=True,
                    stop=True,
                )

        def by_group(ap):
            return ap.rearrange("p r (b j) -> p r b j", j=GROUP)

        def sum_groups(c):
            k, h = divmod(c, 2)
            width = CHUNK // GROUP
            nc.vector.tensor_reduce(
                out=sums[k][:, :, width * h : width * (h + 1)], in_=by_group(z_banks[c][:]), axis=mybir.AxisListType.X, op=ALU.add
            )

        def make_s(k):
            half, pair_in_half = divmod(k, 2)
            width = PAIR // GROUP
            nc.vector.scalar_tensor_tensor(
                out=s_tiles[k][:],
                in0=sums[k][:],
                scalar=1.0 / GROUP,
                in1=g_banks[half][:, :, width * pair_in_half : width * (pair_in_half + 1)],
                op0=ALU.mult,
                op1=ALU.add,
            )

        def make_shared(k):
            nc.scalar.activation(
                out=shared[k][:].rearrange("p h r b -> p r h b"),
                in_=s_tiles[k][:].rearrange("p r (h b) -> p r h b", h=2),
                func=ACT.Relu,
            )

        def result_views(c):
            k, h = divmod(c, 2)
            return (
                by_group(y[k][:, :, CHUNK * h : CHUNK * (h + 1)]),
                shared[k][:, h].unsqueeze(3).to_broadcast([P, PACK, CHUNK // GROUP, GROUP]),
            )

        def result_on_vector(c):
            dst, repeated = result_views(c)
            nc.vector.scalar_tensor_tensor(
                out=dst, in0=by_group(z_banks[c][:]), scalar=Z_SCALE, in1=repeated, op0=ALU.mult, op1=ALU.add
            )

        def scale_z(c):
            nc.scalar.activation(out=z_scaled[c][:], in_=z_banks[c][:], func=ACT.Copy, scale=Z_SCALE)

        def result_on_gpsimd(c):
            dst, repeated = result_views(c)
            nc.gpsimd.tensor_tensor(out=dst, in0=by_group(z_scaled[c][:]), in1=repeated, op=ALU.add)

        def store_y(k):
            nc.sync.dma_start(out=out_0.rearrange("(p r) t -> p r t", r=PACK)[:, :, PAIR * k : PAIR * (k + 1)], in_=y[k][:])

        def store_codes(first_pair, end_pair):
            nc.sync.dma_start(
                out=out_1[0].rearrange("p c r -> p (c r)")[:, PACK * PAIR * first_pair : PACK * PAIR * end_pair].bitcast(I32),
                in_=y_codes[:, PAIR * first_pair : PAIR * end_pair].bitcast(I32),
            )

        def store_plane():
            for q in range(QUADRANTS):
                queue = nc.scalar if q < QUADRANTS // 2 else nc.sync
                queue.dma_start(
                    out=out_2[0, 4 * q : 4 * q + 4, :].bitcast(I32), in_=y_plane[32 * q : 32 * q + 4, :].bitcast(I32)
                )

        nc.gpsimd.memset(wa_raw_plane[:].bitcast(I32), 0)
        nc.vector.memset(xt_plane[:].bitcast(I32), 0)
        nc.gpsimd.memset(xg_plane[:].bitcast(I32), 0)
        nc.gpsimd.memset(wq_raw_plane[:].bitcast(I32), 0)

        nc.sync.dma_start(out=wa_raw[:], in_=wa_words.rearrange("z p n r -> p z (n r)").bitcast(I32))
        load_plane(wa_raw_plane, wa_scales)
        load_xq(0)
        load_xt(0)
        nc.sync.dma_start(out=wq_raw[:].bitcast(I32), in_=wq_words[0].bitcast(I32))
        load_plane(wq_raw_plane, wq_scales, nc.gpsimd, range(QUADRANTS // 2, QUADRANTS))
        load_plane(xt_plane, xt_scales)
        load_xq(1)
        load_plane(wq_raw_plane, wq_scales, nc.sync, range(QUADRANTS // 2))
        load_wg(0)
        load_wg(1)
        load_xq(2)
        nc.sync.dma_start(out=xg_codes[:], in_=xg_words[0].rearrange("p b r -> p (b r)").bitcast(I32))
        load_plane(xg_plane, xg_scales)
        load_xt(1)
        load_xq(3)

        nc.vector.tensor_copy(
            out=wa_codes[:].rearrange("p z (a e m) -> p z a m e", a=2, e=2),
            in_=wa_raw[:].rearrange("p z (m a e) -> p z a m e", a=2, e=2),
        )
        nc.vector.tensor_copy(
            out=wa_plane[:].rearrange("p z (r m) -> p z r m", r=PACK),
            in_=wa_raw_plane[:].rearrange("p z (m r) -> p z r m", r=PACK),
        )
        for h in range(2):
            round_xq(0, h * CHUNK, CHUNK)
        nc.vector.tensor_copy(
            out=wq_codes[:].rearrange("p (r m e) -> p r m e", r=PACK, e=2),
            in_=wq_raw[:].rearrange("p (m r e) -> p r m e", r=PACK, e=2),
        )
        for h in range(2):
            quantise_xq(0, h * CHUNK, CHUNK)
        nc.vector.tensor_copy(
            out=wq_plane[:].rearrange("p (r m) -> p r m", r=PACK),
            in_=wq_raw_plane[:, 0, :].rearrange("p (m r) -> p r m", r=PACK),
        )

        multiply_xt(0)
        multiply_xt(1)
        multiply_xq(0)
        multiply_xq(1)
        round_xq(1)
        quantise_xq(1)
        for c in (2, 3):
            multiply_xt(c)
            multiply_xq(c)

        round_wg(nc.scalar.copy, 0, 0, WG_HALF)
        round_wg(nc.scalar.copy, 1, 0, WG_SCALAR_SHARE)
        sum_groups(0)
        sum_groups(1)
        round_wg(nc.vector.tensor_copy, 1, WG_SCALAR_SHARE, WG_HALF)
        sum_groups(2)
        quantise(wg_codes[:], wg_plane[:], wg_bf[:])
        multiply_xg(0)
        multiply_xt(4)
        multiply_xt(5)
        scale_z(0)
        round_xq(2)
        sum_groups(3)

        make_s(0)
        make_shared(0)
        quantise_xq(2)
        multiply_xq(4)
        multiply_xq(5)
        multiply_xg(1)
        multiply_xt(6)
        make_s(1)
        make_shared(1)
        round_xq(3)
        scale_z(2)

        result_on_gpsimd(0)
        result_on_vector(1)
        store_y(0)
        multiply_xt(7)
        sum_groups(4)
        sum_groups(5)
        quantise_xq(3)
        multiply_xq(6)
        multiply_xq(7)

        result_on_gpsimd(2)
        result_on_vector(3)
        store_y(1)
        scale_z(4)
        make_s(2)
        make_shared(2)
        round_y(nc.scalar.copy, 0)

        result_on_gpsimd(4)
        sum_groups(6)
        sum_groups(7)
        make_s(3)
        make_shared(3)
        round_y(nc.scalar.copy, 1)
        result_on_vector(5)
        store_y(2)
        round_y(nc.scalar.copy, 2)

        result_on_vector(6)
        result_on_vector(7)
        store_y(3)

        quantise_y(0)
        quantise_y(1)
        store_codes(0, 2)
        round_y(nc.vector.tensor_copy, 3)
        quantise_y(2)
        quantise_y(3)
        store_codes(2, PAIRS)
        store_plane()
